import numpy as np
import ml_dtypes

BF16 = ml_dtypes.bfloat16


def bf(x):
    return np.asarray(x, np.float32).astype(BF16)


def f32(x):
    return np.asarray(x, np.float32)


def f64(x):
    return np.asarray(x).astype(np.float64)


def striped(idx):
    return np.tile(idx.reshape(-1, 16).T, (8, 1))


S, K, M, N, V, D = 512, 128, 128, 256, 32, 8


def setup_inputs():
    return {"table": bf(np.random.standard_normal((K, S))), "w": bf(np.random.standard_normal((K, M)) / np.sqrt(K)), "c": f32(1.5 * np.random.standard_normal((1, N))), "b": f32(0.5 * np.random.standard_normal((M, 1))), "offs": striped(np.random.permutation(np.tile(np.arange(S), 2))[:N])}


def reference(table, w, c, b, offs):
    idx = offs[:16].T.reshape(-1)
    y = (f64(w).T @ f64(table)[:, idx]).reshape(M, V, D)
    a = np.exp(f64(c).reshape(V, D))
    a = a / a.sum(axis=1, keepdims=True)
    z = (y * a).sum(axis=2)
    return np.tanh(z + f64(b))

@@ -1,0 +1,64 @@
+import concourse.mybir as mybir
+
+K, S, M, N = 128, 512, 128, 256
+V, D = 32, 8
+LIST_ROWS = 16
+
+FLOPS = 2 * K * M * N
+
+BF16, F32, U16 = mybir.dt.bfloat16, mybir.dt.float32, mybir.dt.uint16
+ALU = mybir.AluOpType
+ACT = mybir.ActivationFunctionType
+INNERMOST = mybir.AxisListType.X
+
+
+def tile_rows_wbag_tanh_rep_kernel(tc, table, w, c, b, offs, out):
+    nc = tc.nc
+    with (
+        tc.tile_pool(name="sbuf", bufs=1) as sbuf,
+        tc.psum_pool(name="psum", bufs=1) as psum,
+    ):
+        nodes = sbuf.tile([K, S], BF16)
+        offsets = sbuf.tile([K, N // LIST_ROWS], U16)
+        weights = sbuf.tile([K, M], BF16)
+        logits = sbuf.tile([M, V, D], F32)
+        bias = sbuf.tile([M, 1], F32)
+        nc.sync.dma_start(nodes[:], table)
+        nc.sync.dma_start(offsets[:], offs)
+        nc.scalar.dma_start(
+            logits[:].rearrange("m v t -> m (v t)"), c[0].partition_broadcast(M)
+        )
+        nc.scalar.dma_start(weights[:], w)
+        nc.scalar.dma_start(bias[:], b)
+
+        top = sbuf.tile([M, V], F32)
+        nc.vector.tensor_reduce(top[:], logits[:], INNERMOST, ALU.max)
+        shifted = sbuf.tile([M, V, D], F32)
+        nc.vector.tensor_tensor(
+            shifted[:], logits[:], top[:].unsqueeze(2).to_broadcast([M, V, D]), ALU.subtract
+        )
+        expd = sbuf.tile([M, V, D], F32)
+        nc.scalar.activation(expd[:], shifted[:], ACT.Exp)
+        total = sbuf.tile([M, V], F32)
+        nc.vector.tensor_reduce(total[:], expd[:], INNERMOST, ALU.add)
+        inverse = sbuf.tile([M, V], F32)
+        nc.vector.reciprocal(inverse[:], total[:])
+        attention = sbuf.tile([M, V, D], F32)
+        nc.vector.tensor_tensor(
+            attention[:], expd[:], inverse[:].unsqueeze(2).to_broadcast([M, V, D]), ALU.mult
+        )
+
+        projected = psum.tile([M, N], F32)
+        nc.tensor.matmul(
+            projected[:], weights[:], nodes[:].indirect(offsets[:]), start=True, stop=True
+        )
+
+        weighted = sbuf.tile([M, V, D], F32)
+        nc.vector.tensor_tensor(
+            weighted[:], projected[:].rearrange("m (v t) -> m v t", t=D), attention[:], ALU.mult
+        )
+        pooled = sbuf.tile([M, V], F32)
+        nc.vector.tensor_reduce(pooled[:], weighted[:], INNERMOST, ALU.add)
+        result = sbuf.tile([M, V], F32)
+        nc.scalar.activation(result[:], pooled[:], ACT.Tanh, bias=bias[:])
+        nc.sync.dma_start(out, result[:])

@@ -2,6 +2,7 @@ import concourse.mybir as mybir
 
 K, S, M, N = 128, 512, 128, 256
 V, D = 32, 8
+BLOCK = 32
 LIST_ROWS = 16
 
 FLOPS = 2 * K * M * N
@@ -14,6 +15,7 @@ INNERMOST = mybir.AxisListType.X
 
 def tile_rows_wbag_tanh_rep_kernel(tc, table, w, c, b, offs, out):
     nc = tc.nc
+    halves = (slice(0, D // 2), slice(D // 2, D))
     with (
         tc.tile_pool(name="sbuf", bufs=1) as sbuf,
         tc.psum_pool(name="psum", bufs=1) as psum,
@@ -21,32 +23,44 @@ def tile_rows_wbag_tanh_rep_kernel(tc, table, w, c, b, offs, out):
         nodes = sbuf.tile([K, S], BF16)
         offsets = sbuf.tile([K, N // LIST_ROWS], U16)
         weights = sbuf.tile([K, M], BF16)
-        logits = sbuf.tile([M, V, D], F32)
+        logits = sbuf.tile([M, D], F32)
         bias = sbuf.tile([M, 1], F32)
+        by_node = c.rearrange("o (v t) -> (o v) t", t=D)
+        for group in range(M // BLOCK):
+            queue = nc.sync if group % 2 == 0 else nc.scalar
+            queue.dma_start(logits[group * BLOCK : (group + 1) * BLOCK, :], by_node)
         nc.sync.dma_start(nodes[:], table)
-        nc.sync.dma_start(offsets[:], offs)
-        nc.scalar.dma_start(
-            logits[:].rearrange("m v t -> m (v t)"), c[0].partition_broadcast(M)
-        )
         nc.scalar.dma_start(weights[:], w)
-        nc.scalar.dma_start(bias[:], b)
+        nc.sync.dma_start(offsets[:], offs)
+        nc.sync.dma_start(bias[:], b)
 
-        top = sbuf.tile([M, V], F32)
-        nc.vector.tensor_reduce(top[:], logits[:], INNERMOST, ALU.max)
-        shifted = sbuf.tile([M, V, D], F32)
-        nc.vector.tensor_tensor(
-            shifted[:], logits[:], top[:].unsqueeze(2).to_broadcast([M, V, D]), ALU.subtract
+        negated = sbuf.tile([M, D], F32)
+        minus_top = sbuf.tile([M, 1], F32)
+        nc.vector.tensor_scalar(
+            negated[:], logits[:], -1.0, None, ALU.mult, ALU.min, accum_out=minus_top[:]
         )
-        expd = sbuf.tile([M, V, D], F32)
-        nc.scalar.activation(expd[:], shifted[:], ACT.Exp)
-        total = sbuf.tile([M, V], F32)
-        nc.vector.tensor_reduce(total[:], expd[:], INNERMOST, ALU.add)
-        inverse = sbuf.tile([M, V], F32)
+        expd = sbuf.tile([M, D], F32)
+        total = sbuf.tile([M, 1], F32)
+        nc.scalar.activation(
+            expd[:], negated[:], ACT.Exp, bias=minus_top[:], scale=-1.0, accum_out=total[:]
+        )
+        inverse = sbuf.tile([M, 1], F32)
         nc.vector.reciprocal(inverse[:], total[:])
-        attention = sbuf.tile([M, V, D], F32)
-        nc.vector.tensor_tensor(
-            attention[:], expd[:], inverse[:].unsqueeze(2).to_broadcast([M, V, D]), ALU.mult
-        )
+        spread = sbuf.tile([M, D, BLOCK], F32, align_bytes=64)
+        attention = sbuf.tile([M, D, V], F32, align_bytes=64)
+        for half in halves:
+            nc.vector.tensor_scalar(
+                spread[:, half, :],
+                expd[:, half].unsqueeze(2).to_broadcast([M, D // 2, BLOCK]),
+                inverse[:],
+                None,
+                ALU.mult,
+            )
+        for half in halves:
+            nc.vector.transpose(
+                attention[:, half, :].rearrange("m t v -> m (t v)"),
+                spread[:, half, :].rearrange("m t i -> m (t i)"),
+            )
 
         projected = psum.tile([M, N], F32)
         nc.tensor.matmul(
@@ -54,9 +68,13 @@ def tile_rows_wbag_tanh_rep_kernel(tc, table, w, c, b, offs, out):
         )
 
         weighted = sbuf.tile([M, V, D], F32)
-        nc.vector.tensor_tensor(
-            weighted[:], projected[:].rearrange("m (v t) -> m v t", t=D), attention[:], ALU.mult
-        )
+        for half in halves:
+            nc.vector.tensor_tensor(
+                weighted[:, :, half],
+                projected[:].rearrange("m (v t) -> m v t", t=D)[:, :, half],
+                attention[:, half, :].rearrange("m t v -> m v t"),
+                ALU.mult,
+            )
         pooled = sbuf.tile([M, V], F32)
         nc.vector.tensor_reduce(pooled[:], weighted[:], INNERMOST, ALU.add)
         result = sbuf.tile([M, V], F32)

@@ -25,10 +25,8 @@ def tile_rows_wbag_tanh_rep_kernel(tc, table, w, c, b, offs, out):
         weights = sbuf.tile([K, M], BF16)
         logits = sbuf.tile([M, D], F32)
         bias = sbuf.tile([M, 1], F32)
-        by_node = c.rearrange("o (v t) -> (o v) t", t=D)
-        for group in range(M // BLOCK):
-            queue = nc.sync if group % 2 == 0 else nc.scalar
-            queue.dma_start(logits[group * BLOCK : (group + 1) * BLOCK, :], by_node)
+        by_node = c.rearrange("o (v t) -> o v t", t=D)
+        nc.sync.dma_start(logits[:], by_node.to_broadcast([M // BLOCK, V, D]))
         nc.sync.dma_start(nodes[:], table)
         nc.scalar.dma_start(weights[:], w)
         nc.sync.dma_start(offsets[:], offs)

@@ -28,7 +28,7 @@ def tile_rows_wbag_tanh_rep_kernel(tc, table, w, c, b, offs, out):
         by_node = c.rearrange("o (v t) -> o v t", t=D)
         nc.sync.dma_start(logits[:], by_node.to_broadcast([M // BLOCK, V, D]))
         nc.sync.dma_start(nodes[:], table)
-        nc.scalar.dma_start(weights[:], w)
+        nc.sync.dma_start(weights[:], w)
         nc.sync.dma_start(offsets[:], offs)
         nc.sync.dma_start(bias[:], b)
 
@@ -66,15 +66,18 @@ def tile_rows_wbag_tanh_rep_kernel(tc, table, w, c, b, offs, out):
         )
 
         weighted = sbuf.tile([M, V, D], F32)
-        for half in halves:
-            nc.vector.tensor_tensor(
-                weighted[:, :, half],
-                projected[:].rearrange("m (v t) -> m v t", t=D)[:, :, half],
-                attention[:, half, :].rearrange("m t v -> m v t"),
-                ALU.mult,
-            )
         pooled = sbuf.tile([M, V], F32)
-        nc.vector.tensor_reduce(pooled[:], weighted[:], INNERMOST, ALU.add)
+        node_halves = (slice(0, V // 2), slice(V // 2, V))
+        for part in node_halves:
+            for half in halves:
+                nc.vector.tensor_tensor(
+                    weighted[:, part, half],
+                    projected[:].rearrange("m (v t) -> m v t", t=D)[:, part, half],
+                    attention[:, half, part].rearrange("m t v -> m v t"),
+                    ALU.mult,
+                )
+        for part in node_halves:
+            nc.vector.tensor_reduce(pooled[:, part], weighted[:, part, :], INNERMOST, ALU.add)
         result = sbuf.tile([M, V], F32)
         nc.scalar.activation(result[:], pooled[:], ACT.Tanh, bias=bias[:])
         nc.sync.dma_start(out, result[:])

import concourse.mybir as mybir

K, S, M, N = 128, 512, 128, 256
V, D = 32, 8
BLOCK = 32
LIST_ROWS = 16

FLOPS = 2 * K * M * N

BF16, F32, U16 = mybir.dt.bfloat16, mybir.dt.float32, mybir.dt.uint16
ALU = mybir.AluOpType
ACT = mybir.ActivationFunctionType
INNERMOST = mybir.AxisListType.X


def tile_rows_wbag_tanh_rep_kernel(tc, table, w, c, b, offs, out):
    nc = tc.nc
    halves = (slice(0, D // 2), slice(D // 2, D))
    with (
        tc.tile_pool(name="sbuf", bufs=1) as sbuf,
        tc.psum_pool(name="psum", bufs=1) as psum,
    ):
        nodes = sbuf.tile([K, S], BF16)
        offsets = sbuf.tile([K, N // LIST_ROWS], U16)
        weights = sbuf.tile([K, M], BF16)
        logits = sbuf.tile([M, D], F32)
        bias = sbuf.tile([M, 1], F32)
        by_node = c.rearrange("o (v t) -> o v t", t=D)
        nc.sync.dma_start(logits[:], by_node.to_broadcast([M // BLOCK, V, D]))
        nc.sync.dma_start(nodes[:], table)
        nc.sync.dma_start(weights[:], w)
        nc.sync.dma_start(offsets[:], offs)
        nc.sync.dma_start(bias[:], b)

        negated = sbuf.tile([M, D], F32)
        minus_top = sbuf.tile([M, 1], F32)
        nc.vector.tensor_scalar(
            negated[:], logits[:], -1.0, None, ALU.mult, ALU.min, accum_out=minus_top[:]
        )
        expd = sbuf.tile([M, D], F32)
        total = sbuf.tile([M, 1], F32)
        nc.scalar.activation(
            expd[:], negated[:], ACT.Exp, bias=minus_top[:], scale=-1.0, accum_out=total[:]
        )
        inverse = sbuf.tile([M, 1], F32)
        nc.vector.reciprocal(inverse[:], total[:])
        spread = sbuf.tile([M, D, BLOCK], F32, align_bytes=64)
        attention = sbuf.tile([M, D, V], F32, align_bytes=64)
        for half in halves:
            nc.vector.tensor_scalar(
                spread[:, half, :],
                expd[:, half].unsqueeze(2).to_broadcast([M, D // 2, BLOCK]),
                inverse[:],
                None,
                ALU.mult,
            )
        for half in halves:
            nc.vector.transpose(
                attention[:, half, :].rearrange("m t v -> m (t v)"),
                spread[:, half, :].rearrange("m t i -> m (t i)"),
            )

        projected = psum.tile([M, N], F32)
        nc.tensor.matmul(
            projected[:], weights[:], nodes[:].indirect(offsets[:]), start=True, stop=True
        )

        weighted = sbuf.tile([M, V, D], F32)
        pooled = sbuf.tile([M, V], F32)
        node_halves = (slice(0, V // 2), slice(V // 2, V))
        for part in node_halves:
            for half in halves:
                nc.vector.tensor_tensor(
                    weighted[:, part, half],
                    projected[:].rearrange("m (v t) -> m v t", t=D)[:, part, half],
                    attention[:, half, part].rearrange("m t v -> m v t"),
                    ALU.mult,
                )
        for part in node_halves:
            nc.vector.tensor_reduce(pooled[:, part], weighted[:, part, :], INNERMOST, ALU.add)
        result = sbuf.tile([M, V], F32)
        nc.scalar.activation(result[:], pooled[:], ACT.Tanh, bias=bias[:])
        nc.sync.dma_start(out, result[:])
